import numpy as np, ml_dtypes
CORES = [23,119,17,113]
N = 4
import mx_ref
BF = ml_dtypes.bfloat16
def entries(a):
    return np.ascontiguousarray(a.T).reshape(-1)
def table(e):
    return np.ascontiguousarray(np.reshape(e, (-1, 16)).T).astype(np.int32)
def cols(t, e):
    v = np.concatenate([t.reshape(128, -1, 4), np.zeros((128, 1, 4), BF)], axis=1)
    return np.ascontiguousarray(v[:, e]).reshape(128, -1)
def f(rng, *shape):
    return mx_ref.flush((rng.standard_normal(shape, dtype=np.float32) * np.exp2(rng.integers(-2, 3, shape[:-1] + (1,)))).astype(BF))
def wide(rng, *shape, cols=0):
    v = rng.standard_normal(shape, dtype=np.float32) * np.exp2(rng.integers(-12, 13, shape)).astype(np.float32)
    if cols: v *= np.repeat(np.exp2(rng.integers(-cols, cols + 1, shape[:-2] + (1, shape[-1] // 4))) * (rng.random(shape[:-2] + (1, shape[-1] // 4)) > 0.0625), 4, axis=-1).astype(np.float32)
    return mx_ref.flush(v.astype(BF))
T, CAPP = 512, 192
def lists(rng, full=False, skew=False, single=False, back=False):
    if full:
        v = rng.permutation(([CAPP] * (T // CAPP) + [T % CAPP] + [0] * N)[:N])
        n = v[(np.arange(N)[None, :] - np.arange(N)[:, None]) % N][rng.permutation(N)][:, rng.permutation(N)]
    else:
        n = np.full((N, N), T // N)
        for _ in range(20 * N):
            (s, t), (d, e) = rng.permutation(N)[:2], rng.permutation(N)[:2]
            k = rng.integers(0, min(n[s, d], n[t, e], CAPP - n[s, e], CAPP - n[t, d]) + 1)
            n[s, d] -= k; n[t, e] -= k; n[s, e] += k; n[t, d] += k
    a = np.full((N, N * CAPP), -1)
    for s in range(N):
        parts = np.split(rng.permutation(T), np.cumsum(n[s])[:-1])
        for d in range(N): a[s, d * CAPP + rng.permutation(CAPP)[:n[s, d]]] = parts[d]
    p, u, o = [], [], []
    for r in range(N):
        used = np.flatnonzero(a[:, r * CAPP:(r + 1) * CAPP].reshape(-1) >= 0)
        p.append(table(used[::-1] if back else rng.permutation(used)))
        h = rng.integers(0, N)
        c = rng.integers(0, 2, N) if full else (np.full(N, -1) if rng.random() < 0.5 else rng.integers(0, 2, N)) if single else rng.integers(-1, 2, N)
        if c[h] < 0: c[h] = rng.integers(0, 2)
        named = np.flatnonzero(c >= 0)
        if single: named = np.array([h])
        if skew:
            m = rng.integers(T // 2 + 1, T + 1)
            e = np.sort(np.concatenate([np.full(m, h), rng.choice(named, T - m)]))
        elif full: e = np.sort(np.concatenate([named, rng.choice(named, T - N)]))
        else: e = np.repeat(named, np.diff(np.concatenate([[0], np.sort(rng.integers(0, T + 1, len(named) - 1)), [T]])))
        u.append(table(np.concatenate([c, np.full(16 - N, -1)]))); o.append(table(e))
    return {"send": np.stack([table(k) for k in a]), "place": np.stack(p), "sel": np.stack(u), "of": np.stack(o)}
def setup_inputs(rng):
    return {"x": f(rng, N, 128, 4 * T), "w": f(rng, N, 256, 512), **lists(rng)}
def setup_inputs_full(rng):
    return {**setup_inputs(rng), **lists(rng, full=True)}
def setup_inputs_reversed(rng):
    return {**setup_inputs(rng), **lists(rng, back=True)}
def setup_inputs_single(rng):
    return {**setup_inputs(rng), **lists(rng, single=True)}
def setup_inputs_skew(rng):
    return {**setup_inputs(rng), **lists(rng, skew=True)}
def setup_inputs_spread(rng):
    d = setup_inputs(rng); d["x"] = wide(rng, N, 128, 4 * T, cols=8); return d
def check_inputs(d):
    b = []
    for k in ("x", "w"):
        a = np.abs(d[k].astype(np.float32))
        if not ((a == 0) | ((a >= 2.0 ** -30) & (a <= 2.0 ** 30))).all(): b.append(k)
    sends = np.stack([entries(d["send"][r]) for r in range(N)])
    for r in range(N):
        c, p, u, e = sends[r], entries(d["place"][r]), entries(d["sel"][r]), entries(d["of"][r])
        if c.min() < -1 or not np.array_equal(np.sort(c[c >= 0]), np.arange(T)): b.append("send")
        if not np.array_equal(np.sort(p), np.flatnonzero(sends[:, r * CAPP:(r + 1) * CAPP].reshape(-1) >= 0)): b.append("place")
        if u.min() < -1 or u.max() > 1 or (u[N:] != -1).any(): b.append("sel")
        if e.min() < 0 or e.max() >= N or (np.diff(e) < 0).any() or (u[e] < 0).any(): b.append("of")
    return b
def reference(x, w, send, place, sel, of):
    W = [[mx_ref.quantize(w[h][128 * m:128 * m + 128]) for m in range(2)] for h in range(N)]
    y = np.zeros((N, 128, T), np.float32)
    for r in range(N):
        slots = np.concatenate([cols(x[s], entries(send[s])[r * CAPP:(r + 1) * CAPP]) for s in range(N)], axis=1)
        X = mx_ref.quantize(cols(slots, entries(place[r])))
        u, e = entries(sel[r]), entries(of[r])
        for h in range(N):
            i = e == h
            if i.any(): y[r][:, i] = mx_ref.matmul(W[h][u[h]], X)[:, i]
    return {"y": y}

@@ -1,0 +1,275 @@
+from concourse.bass import DstId, RemoteDMATransfer
+from concourse.mybir import dt, AluOpType, ActivationFunctionType
+
+CAP = 192
+NX = 512
+EX = 128
+SL = 4 * CAP
+RUN = CAP + EX
+
+L_EP, L_P, L_O, L_A, L_B, L_EB = 0, EX, EX + CAP, EX + 2 * CAP, EX + 3 * CAP, EX + 4 * CAP
+L_N = 2 * EX + SL
+BL_O, BL_A, BL_P, BL_B = 0, 1, 3, 4
+
+CODE = "float8_e4m3fn_x4"
+SCRATCH = {
+    "raws": ("sbuf", [32, 48], "int32"),
+    "rawp": ("sbuf", [32, 32], "int32"),
+    "rawo": ("sbuf", [32, 32], "int32"),
+    "selr": ("sbuf", [128, 16], "int32"),
+    "self1": ("sbuf", [128, 16], "float32"),
+    "selm": ("sbuf", [128, 16], "float32"),
+    "sela": ("sbuf", [128, 1], "float32"),
+    "ia": ("sbuf", [128, 32], "int32"),
+    "ib": ("sbuf", [128, 32], "int32"),
+    "ic": ("sbuf", [128, 32], "int32"),
+    "base": ("sbuf", [128, 32], "float32"),
+    "off": ("sbuf", [128, 48], "uint16"),
+    "offo": ("sbuf", [128, 32], "uint16"),
+    "offp": ("sbuf", [128, 32], "uint16"),
+    "offb": ("sbuf", [128, 32], "uint16"),
+    "offy": ("sbuf", [128, 32], "uint16"),
+    "tm": ("sbuf", [32, 256], "float32"),
+    "tn": ("sbuf", [32, 128], "float32"),
+    "to": ("sbuf", [32, 64], "float32"),
+    "tp": ("sbuf", [32, 32], "float32"),
+    "msgp": ("sbuf", [128, 1], "float32"),
+    "msgb": ("sbuf", [128, 1], "float32"),
+    "xt": ("sbuf", [128, 4 * NX], "bfloat16"),
+    "wt": ("sbuf", [128, 8 * EX], "bfloat16"),
+    "ho": ("sbuf", [128, 4 * EX], "bfloat16"),
+    "ha": ("sbuf", [128, 4 * CAP], "bfloat16"),
+    "hp": ("sbuf", [128, 4 * RUN], "bfloat16"),
+    "hb": ("sbuf", [128, 4 * RUN], "bfloat16"),
+    "hx": ("sbuf", [128, 4 * CAP], "bfloat16"),
+    "qe": ("sbuf", [128, 2 * EX], CODE), "se": ("sbuf", [128, 2 * EX], "uint8"),
+    "qo": ("sbuf", [128, EX], CODE), "so": ("sbuf", [128, EX], "uint8"),
+    "qa": ("sbuf", [128, CAP], CODE), "sa": ("sbuf", [128, CAP], "uint8"),
+    "qp": ("sbuf", [128, RUN], CODE), "sp": ("sbuf", [128, RUN], "uint8"),
+    "qb": ("sbuf", [128, RUN], CODE), "sb": ("sbuf", [128, RUN], "uint8"),
+    "le": ("sbuf", [128, 2 * EX], CODE), "les": ("sbuf", [128, 2 * EX], "uint8"),
+    "lc": ("sbuf", [128, L_N], CODE), "lcs": ("sbuf", [128, L_N], "uint8"),
+    "win": ("sbuf", [128, 5 * SL], "float32"),
+    "yt": ("sbuf", [128, NX], "float32"),
+}
+for _k in range(8):
+    SCRATCH["ps%d" % _k] = ("psum", [128, 512], "float32")
+
+SEMAPHORES = ["ld_sel", "ld_send", "ld_w", "ld_x", "ld_pl", "st_a", "st_b",
+              "io", "io2", "bas", "sf", "sm", "off", "offo", "offp", "offb", "offy", "sel_a",
+              "tmd", "tnd", "tod", "tpd",
+              "q_e", "q_o", "q_a", "q_p", "q_b", "q_x",
+              "g_o", "g_a", "g_p", "g_b", "g_x", "g_y1", "g_y2",
+              "sent", "a_mp", "a_mb", "a_e", "a_a", "a_p", "a_b",
+              "ev1", "ev2", "ev3"] + ["mm%d" % k for k in range(14)]
+
+
+def rank_program(g, core, T, topo):
+    rank = T.rank_of(core)
+    if rank is None:
+        return
+    S = T.sem
+    V, A_, TE, SY = g.vector, g.scalar, g.tensor, g.sync
+    op = AluOpType
+    copy = ActivationFunctionType.Copy
+
+    others = [d for d in range(len(T.cores)) if d != rank]
+    P = [d for d in others if topo.chip(T.cores[d]) == topo.chip(core)][0]
+    far = [d for d in others if d != P]
+    B = [d for d in far if topo.die(T.cores[d]) == topo.die(core)][0]
+    A = [d for d in far if d != B][0]
+    eng_far = topo.engines(core, T.cores[B])
+    eng_p = [e for e in topo.engines(core, T.cores[P]) if e not in eng_far]
+    m_far = sum(1 << e for e in eng_far)
+    m_p = sum(1 << e for e in eng_p)
+
+    def dst(d):
+        rid, pid, _ = topo.addr(T.cores[d])
+        return rid, pid
+
+    def vec(inst, sem, n=1):
+        inst.then_inc(S[sem], n)
+
+    SY.dma_start(T.selr[0:1, 0:16], T.sel[:]).then_inc(S.ld_sel, 16)
+    A_.dma_start(T.raws[0:16, :], T.send[:]).then_inc(S.ld_send, 16)
+    SY.dma_start(T.wt[:, 0:4 * EX], T.w[0:128, :]).then_inc(S.ld_w, 16)
+    A_.dma_start(T.raws[16:32, :], T.send[:]).then_inc(S.ld_send, 16)
+    A_.dma_start(T.wt[:, 4 * EX:8 * EX], T.w[128:256, :]).then_inc(S.ld_w, 16)
+    SY.dma_start(T.xt[:], T.x[:]).then_inc(S.ld_x, 16)
+    for k in range(2):
+        SY.dma_start(T.rawp[16 * k:16 * k + 16, :], T.place[:]).then_inc(S.ld_pl, 16)
+        SY.dma_start(T.rawo[16 * k:16 * k + 16, :], T.of[:]).then_inc(S.ld_pl, 16)
+
+    g.iota(T.ia[:], [[16, 32]], 0, 1).then_inc(S["io"], 1)
+    g.iota(T.ic[:], [[16, 32]], 0, 0).then_inc(S.io2, 1)
+    V.wait_ge(S["io"], 1)
+    vec(V.tensor_scalar(T.ib[:], T.ia[:], 15, None, op.bitwise_and), "bas")
+    V.wait_ge(S["bas"], 1)
+    V.wait_ge(S.io2, 1)
+    vec(V.tensor_tensor(T.base[:], T.ib[:], T.ic[:], op.add), "bas")
+
+    V.wait_ge(S.ld_sel, 16)
+    vec(V.tensor_scalar(T.self1[0:1, :], T.selr[0:1, :], 0.0, float(4 * EX), op.max, op.mult), "sf")
+    g.wait_ge(S.sf, 1)
+    g.partition_broadcast(T.selm[:], T.self1[0:1, :], 128).then_inc(S.sm, 1)
+    g.wait_ge(S.sm, 1)
+    rb, pb = dst(B)
+    rp, pp = dst(P)
+    g.remote_dma_fused([
+        RemoteDMATransfer(dst_ids=[DstId(rid=rb, pnc=pb)], dma_engine_mask=m_far, remote_sem=S.a_mb,
+                          src=T.selm[:, B:B + 1], dst=T.msgb[:]),
+        RemoteDMATransfer(dst_ids=[DstId(rid=rp, pnc=pp)], dma_engine_mask=m_p, remote_sem=S.a_mp,
+                          src=T.selm[:, P:P + 1], dst=T.msgp[:]),
+    ], local_sem=S.sent)
+    n_sent = [len(eng_far) + len(eng_p)]
+
+    def ship(d, lq, ls, l0, q, s, n, rsem, mask, cnt):
+        rid, pid = dst(d)
+        g.remote_dma(lq[:, l0:l0 + n].bitcast(dt.uint8), q[:, 0:n].bitcast(dt.uint8), rsem, S.sent, pid, rid, mask)
+        g.remote_dma(ls[:, l0:l0 + n], s[:, 0:n], rsem, S.sent, pid, rid, mask)
+        n_sent[0] += 2 * cnt
+
+    V.wait_ge(S.ld_send, 32)
+    for a in range(4):
+        vec(V.tensor_scalar(T.off[32 * a:32 * a + 32, :], T.raws[:], 4.0, 0.0, op.mult, op.max), "off")
+    V.wait_ge(S.ld_w, 32)
+    vec(V.quantize_mx(T.qe[:], T.se[:], T.wt[:]), "q_e")
+    g.wait_ge(S.q_e, 1)
+    nf, npe = len(eng_far), len(eng_p)
+    ship(A, T.le, T.les, 0, T.qe, T.se, 2 * EX, S.a_e, m_far, nf)
+
+    V.wait_ge(S.bas, 2)
+    V.wait_ge(S.sm, 1)
+    vec(V.tensor_scalar(T.offo[:], T.base[:], T.selm[:, rank:rank + 1], None, op.add), "offo")
+    for q in (V, A_):
+        q.wait_ge(S.offo, 1)
+        q.wait_ge(S.ld_w, 32)
+    H = 2 * EX
+    vec(V.tensor_copy(T.ho[:, 0:H], T.wt[:].indirect(T.offo[:, 0:16])), "g_o")
+    vec(A_.activation(T.ho[:, H:2 * H], T.wt[:].indirect(T.offo[:, 16:32]), copy), "g_o")
+
+    def cols(tile, e0, d, ts_v, ts_s, sem):
+        o = T.off[:, 12 * d:12 * d + 12]
+        for t in ts_v:
+            vec(V.tensor_copy(tile[:, e0 + t:e0 + 4 * CAP:4], T.xt[:, t:4 * NX].indirect(o)), sem)
+        for t in ts_s:
+            vec(A_.activation(tile[:, e0 + t:e0 + 4 * CAP:4], T.xt[:, t:4 * NX].indirect(o), copy), sem)
+
+    for q in (V, A_):
+        q.wait_ge(S.off, 4)
+        q.wait_ge(S.ld_x, 16)
+    cols(T.ha, 0, A, (0, 1), (2, 3), "g_a")
+    V.wait_ge(S.g_a, 4)
+    vec(V.quantize_mx(T.qa[:], T.sa[:], T.ha[:]), "q_a")
+    g.wait_ge(S.q_a, 1)
+    ship(A, T.lc, T.lcs, L_A, T.qa, T.sa, CAP, S.a_a, m_far, nf)
+
+    cols(T.hp, 4 * EX, P, (0, 1), (2, 3), "g_p")
+    cols(T.hb, 0, B, (0, 1), (2, 3), "g_b")
+    V.wait_ge(S.a_mp, npe)
+    vec(V.tensor_scalar(T.offp[:], T.base[:], T.msgp[:], None, op.add), "offp")
+    V.wait_ge(S.a_mb, nf)
+    vec(V.tensor_scalar(T.offb[:], T.base[:], T.msgb[:], None, op.add), "offb")
+    V.wait_ge(S.offp, 1)
+    A_.wait_ge(S.offp, 1)
+    vec(V.tensor_copy(T.hp[:, 0:H], T.wt[:].indirect(T.offp[:, 0:16])), "g_p")
+    vec(A_.activation(T.hp[:, H:2 * H], T.wt[:].indirect(T.offp[:, 16:32]), copy), "g_p")
+    A_.wait_ge(S.offb, 1)
+    vec(A_.activation(T.hb[:, 4 * CAP:4 * RUN], T.wt[:].indirect(T.offb[:]), copy), "g_b")
+    V.wait_ge(S.g_p, 6)
+    vec(V.quantize_mx(T.qp[:], T.sp[:], T.hp[:]), "q_p")
+    g.wait_ge(S.q_p, 1)
+    ship(P, T.lc, T.lcs, L_EP, T.qp, T.sp, RUN, S.a_p, m_p, npe)
+    V.wait_ge(S.g_b, 5)
+    vec(V.quantize_mx(T.qb[:], T.sb[:], T.hb[:]), "q_b")
+    g.wait_ge(S.q_b, 1)
+    ship(B, T.lc, T.lcs, L_B, T.qb, T.sb, RUN, S.a_b, m_far, nf)
+    cols(T.hx, 0, rank, (0, 1), (2, 3), "g_x")
+    V.wait_ge(S.g_o, 2)
+    vec(V.quantize_mx(T.qo[:], T.so[:], T.ho[:]), "q_o")
+    V.wait_ge(S.g_x, 4)
+    vec(V.quantize_mx(T.lc[:, L_O:L_O + CAP], T.lcs[:, L_O:L_O + CAP], T.hx[:]), "q_x")
+
+    pos = {P: 0, rank: 1, A: 2, B: 3}
+    blk = {rank: BL_O, A: BL_A, P: BL_P, B: BL_B}
+    V.wait_ge(S.ld_pl, 64)
+    vec(V.tensor_scalar(T.sela[:], T.selm[:, A:A + 1], float(SL) / (4 * EX), None, op.mult), "sel_a")
+    vec(V.tensor_scalar(T.tm[:, 0:32], T.rawp[:], float(CAP * pos[0] + SL * blk[0]), None, op.add), "tmd")
+    for k in range(1, 4):
+        vec(V.tensor_scalar(T.tm[:, 32 * k:32 * k + 32], T.rawp[:], float(CAP * k),
+                            float(CAP * (pos[k] - pos[k - 1] - 1)), op.is_ge, op.mult), "tmd")
+        vec(V.tensor_scalar(T.tm[:, 96 + 32 * k:128 + 32 * k], T.rawo[:], float(k),
+                            float(SL * (blk[k] - blk[k - 1])), op.is_ge, op.mult), "tmd")
+    V.wait_ge(S.sel_a, 1)
+    vec(V.tensor_scalar(T.tm[:, 224:256], T.rawo[:], float(A), T.sela[0:32, :], op.is_equal, op.mult), "tmd")
+    V.wait_ge(S.tmd, 8)
+    vec(V.tensor_tensor(T.tn[:], T.tm[:, 0:128], T.tm[:, 128:256], op.add), "tnd")
+    V.wait_ge(S.tnd, 1)
+    vec(V.tensor_tensor(T.to[:], T.tn[:, 0:64], T.tn[:, 64:128], op.add), "tod")
+    V.wait_ge(S.tod, 1)
+    vec(V.tensor_tensor(T.tp[:], T.to[:, 0:32], T.to[:, 32:64], op.add), "tpd")
+    V.wait_ge(S.tpd, 1)
+    for a in range(4):
+        vec(V.tensor_copy(T.offy[32 * a:32 * a + 32, :], T.tp[:]), "offy")
+
+    own = (T.qo, T.so, 0, BL_O)
+    a0 = (T.le, T.les, 0, BL_A)
+    a1 = (T.le, T.les, EX, BL_A + 1)
+    ep = (T.lc, T.lcs, L_EP, BL_P)
+    eb = (T.lc, T.lcs, L_EB, BL_B)
+    nmm = [0]
+
+    def prod(e, c0, c1, bank, eng, ev):
+        q, s, j, b = e
+        k = nmm[0]
+        nmm[0] += 1
+        ps = T["ps%d" % bank]
+        sem = S["mm%d" % k]
+        TE.matmul_mx(ps[:, 0:c1 - c0], q[:, j:j + EX], s[:, j:j + EX], T.lc[:, c0:c1], T.lcs[:, c0:c1],
+                     True, True).then_inc(sem, 1)
+        w0 = SL * b + c0 - L_P
+        eng.wait_ge(sem, 1)
+        if eng is V:
+            V.tensor_copy(T.win[:, w0:w0 + c1 - c0], ps[:, 0:c1 - c0]).then_inc(S[ev], 1)
+        else:
+            A_.activation(T.win[:, w0:w0 + c1 - c0], ps[:, 0:c1 - c0], copy).then_inc(S[ev], 1)
+
+    TE.wait_ge(S.q_o, 1)
+    TE.wait_ge(S.q_x, 1)
+    TE.wait_ge(S.a_e, 2 * nf)
+    TE.wait_ge(S.a_a, 2 * nf)
+    prod(own, L_O, L_B, 0, A_, "ev1")
+    prod(a0, L_O, L_B, 1, V, "ev1")
+    prod(a1, L_O, L_B, 2, A_, "ev1")
+    TE.wait_ge(S.a_p, 2 * npe)
+    mid = L_P + 3 * CAP // 2
+    prod(ep, L_P, mid, 6, V, "ev2")
+    prod(ep, mid, L_B, 7, A_, "ev2")
+    prod(own, L_P, L_O, 3, V, "ev2")
+    prod(a0, L_P, L_O, 4, A_, "ev2")
+    prod(a1, L_P, L_O, 5, V, "ev2")
+    TE.wait_ge(S.a_b, 2 * nf)
+    TE.wait_ge(S.ev1, 3)
+    prod(eb, L_P, L_A, 0, V, "ev3")
+    prod(eb, L_A, L_EB, 1, A_, "ev3")
+    prod(own, L_B, L_EB, 2, V, "ev3")
+    TE.wait_ge(S.ev2, 5)
+    prod(a0, L_B, L_EB, 3, A_, "ev3")
+    prod(a1, L_B, L_EB, 4, V, "ev3")
+    prod(ep, L_B, L_EB, 5, A_, "ev3")
+
+    for q in (V, A_):
+        q.wait_ge(S.offy, 4)
+        q.wait_ge(S.ev1, 3)
+        q.wait_ge(S.ev2, 5)
+        q.wait_ge(S.ev3, 6)
+    h = NX // 2
+    V.tensor_copy(T.yt[:, 0:h], T.win[:].indirect(T.offy[:, 0:16])).then_inc(S.g_y1, 1)
+    A_.activation(T.yt[:, h:NX], T.win[:].indirect(T.offy[:, 16:32]), copy).then_inc(S.g_y2, 1)
+    SY.wait_ge(S.g_y1, 1)
+    SY.dma_start(T.y[:, 0:h], T.yt[:, 0:h]).then_inc(S.st_a, 16)
+    A_.wait_ge(S.g_y2, 1)
+    A_.dma_start(T.y[:, h:NX], T.yt[:, h:NX]).then_inc(S.st_b, 16)
+    SY.wait_ge(S.st_a, 16)
+    A_.wait_ge(S.st_b, 16)
+    g.wait_ge(S.sent, n_sent[0])

@@ -5,11 +5,10 @@ CAP = 192
 NX = 512
 EX = 128
 SL = 4 * CAP
-RUN = CAP + EX
+EV, OV = 4 * EX, 4 * CAP
 
-L_EP, L_P, L_O, L_A, L_B, L_EB = 0, EX, EX + CAP, EX + 2 * CAP, EX + 3 * CAP, EX + 4 * CAP
-L_N = 2 * EX + SL
-BL_O, BL_A, BL_P, BL_B = 0, 1, 3, 4
+E_A, E_B, E_P = 0, 2 * EX, 3 * EX
+SECOND = 4
 
 CODE = "float8_e4m3fn_x4"
 SCRATCH = {
@@ -29,26 +28,26 @@ SCRATCH = {
     "offp": ("sbuf", [128, 32], "uint16"),
     "offb": ("sbuf", [128, 32], "uint16"),
     "offy": ("sbuf", [128, 32], "uint16"),
-    "tm": ("sbuf", [32, 256], "float32"),
-    "tn": ("sbuf", [32, 128], "float32"),
-    "to": ("sbuf", [32, 64], "float32"),
-    "tp": ("sbuf", [32, 32], "float32"),
+    "t1": ("sbuf", [32, 32], "float32"),
+    "t2": ("sbuf", [32, 32], "float32"),
+    "t3": ("sbuf", [32, 32], "float32"),
+    "t4": ("sbuf", [32, 32], "float32"),
     "msgp": ("sbuf", [128, 1], "float32"),
     "msgb": ("sbuf", [128, 1], "float32"),
     "xt": ("sbuf", [128, 4 * NX], "bfloat16"),
-    "wt": ("sbuf", [128, 8 * EX], "bfloat16"),
-    "ho": ("sbuf", [128, 4 * EX], "bfloat16"),
-    "ha": ("sbuf", [128, 4 * CAP], "bfloat16"),
-    "hp": ("sbuf", [128, 4 * RUN], "bfloat16"),
-    "hb": ("sbuf", [128, 4 * RUN], "bfloat16"),
-    "hx": ("sbuf", [128, 4 * CAP], "bfloat16"),
+    "wt": ("sbuf", [128, 2 * EV], "bfloat16"),
+    "ho": ("sbuf", [128, EV], "bfloat16"),
+    "he": ("sbuf", [128, 2 * EV], "bfloat16"),
+    "ha": ("sbuf", [128, OV], "bfloat16"),
+    "hbp": ("sbuf", [128, 2 * OV], "bfloat16"),
+    "hx": ("sbuf", [128, OV], "bfloat16"),
+    "qw": ("sbuf", [128, 2 * EX], CODE), "sw": ("sbuf", [128, 2 * EX], "uint8"),
     "qe": ("sbuf", [128, 2 * EX], CODE), "se": ("sbuf", [128, 2 * EX], "uint8"),
     "qo": ("sbuf", [128, EX], CODE), "so": ("sbuf", [128, EX], "uint8"),
     "qa": ("sbuf", [128, CAP], CODE), "sa": ("sbuf", [128, CAP], "uint8"),
-    "qp": ("sbuf", [128, RUN], CODE), "sp": ("sbuf", [128, RUN], "uint8"),
-    "qb": ("sbuf", [128, RUN], CODE), "sb": ("sbuf", [128, RUN], "uint8"),
-    "le": ("sbuf", [128, 2 * EX], CODE), "les": ("sbuf", [128, 2 * EX], "uint8"),
-    "lc": ("sbuf", [128, L_N], CODE), "lcs": ("sbuf", [128, L_N], "uint8"),
+    "qbp": ("sbuf", [128, 2 * CAP], CODE), "sbp": ("sbuf", [128, 2 * CAP], "uint8"),
+    "le": ("sbuf", [128, 4 * EX], CODE), "les": ("sbuf", [128, 4 * EX], "uint8"),
+    "lc": ("sbuf", [128, SL], CODE), "lcs": ("sbuf", [128, SL], "uint8"),
     "win": ("sbuf", [128, 5 * SL], "float32"),
     "yt": ("sbuf", [128, NX], "float32"),
 }
@@ -57,11 +56,11 @@ for _k in range(8):
 
 SEMAPHORES = ["ld_sel", "ld_send", "ld_w", "ld_x", "ld_pl", "st_a", "st_b",
               "io", "io2", "bas", "sf", "sm", "off", "offo", "offp", "offb", "offy", "sel_a",
-              "tmd", "tnd", "tod", "tpd",
-              "q_e", "q_o", "q_a", "q_p", "q_b", "q_x",
-              "g_o", "g_a", "g_p", "g_b", "g_x", "g_y1", "g_y2",
-              "sent", "a_mp", "a_mb", "a_e", "a_a", "a_p", "a_b",
-              "ev1", "ev2", "ev3"] + ["mm%d" % k for k in range(14)]
+              "t1d", "t2d", "t3d", "t4d",
+              "q_w", "q_e", "q_o", "q_a", "q_bp", "q_x",
+              "g_o", "g_a", "g_bp", "g_e", "g_x", "g_y1", "g_y2",
+              "sent", "a_mp", "a_mb", "a_e", "a_a", "a_p", "a_b", "a_eb", "a_ep",
+              "ev1", "ev2", "ev3", "ev4"] + ["mm%d" % k for k in range(10)]
 
 
 def rank_program(g, core, T, topo):
@@ -76,12 +75,16 @@ def rank_program(g, core, T, topo):
     others = [d for d in range(len(T.cores)) if d != rank]
     P = [d for d in others if topo.chip(T.cores[d]) == topo.chip(core)][0]
     far = [d for d in others if d != P]
-    B = [d for d in far if topo.die(T.cores[d]) == topo.die(core)][0]
-    A = [d for d in far if d != B][0]
+    A = [d for d in far if topo.die(T.cores[d]) == topo.die(core)][0]
+    B = [d for d in far if d != A][0]
+    assert abs(rank - A) == 1 and abs(B - P) == 1
+    oa, bp = min(rank, A), min(B, P)
+    jb, jp = CAP * (B - bp), CAP * (P - bp)
     eng_far = topo.engines(core, T.cores[B])
     eng_p = [e for e in topo.engines(core, T.cores[P]) if e not in eng_far]
     m_far = sum(1 << e for e in eng_far)
     m_p = sum(1 << e for e in eng_p)
+    nf, npe = len(eng_far), len(eng_p)
 
     def dst(d):
         rid, pid, _ = topo.addr(T.cores[d])
@@ -91,14 +94,15 @@ def rank_program(g, core, T, topo):
         inst.then_inc(S[sem], n)
 
     SY.dma_start(T.selr[0:1, 0:16], T.sel[:]).then_inc(S.ld_sel, 16)
-    A_.dma_start(T.raws[0:16, :], T.send[:]).then_inc(S.ld_send, 16)
-    SY.dma_start(T.wt[:, 0:4 * EX], T.w[0:128, :]).then_inc(S.ld_w, 16)
     A_.dma_start(T.raws[16:32, :], T.send[:]).then_inc(S.ld_send, 16)
-    A_.dma_start(T.wt[:, 4 * EX:8 * EX], T.w[128:256, :]).then_inc(S.ld_w, 16)
-    SY.dma_start(T.xt[:], T.x[:]).then_inc(S.ld_x, 16)
+    SY.dma_start(T.raws[0:16, :], T.send[:]).then_inc(S.ld_send, 16)
+    A_.dma_start(T.rawp[0:16, :], T.place[:]).then_inc(S.ld_pl, 16)
+    SY.dma_start(T.rawp[16:32, :], T.place[:]).then_inc(S.ld_pl, 16)
+    A_.dma_start(T.rawo[0:16, :], T.of[:]).then_inc(S.ld_pl, 16)
     for k in range(2):
-        SY.dma_start(T.rawp[16 * k:16 * k + 16, :], T.place[:]).then_inc(S.ld_pl, 16)
-        SY.dma_start(T.rawo[16 * k:16 * k + 16, :], T.of[:]).then_inc(S.ld_pl, 16)
+        SY.dma_start(T.wt[:, EV * k:EV * k + EV], T.w[128 * k:128 * k + 128, :]).then_inc(S.ld_w, 16)
+    A_.dma_start(T.rawo[16:32, :], T.of[:]).then_inc(S.ld_pl, 16)
+    SY.dma_start(T.xt[:], T.x[:]).then_inc(S.ld_x, 16)
 
     g.iota(T.ia[:], [[16, 32]], 0, 1).then_inc(S["io"], 1)
     g.iota(T.ic[:], [[16, 32]], 0, 0).then_inc(S.io2, 1)
@@ -109,160 +113,155 @@ def rank_program(g, core, T, topo):
     vec(V.tensor_tensor(T.base[:], T.ib[:], T.ic[:], op.add), "bas")
 
     V.wait_ge(S.ld_sel, 16)
-    vec(V.tensor_scalar(T.self1[0:1, :], T.selr[0:1, :], 0.0, float(4 * EX), op.max, op.mult), "sf")
+    vec(V.tensor_scalar(T.self1[0:1, :], T.selr[0:1, :], 0.0, float(EV), op.max, op.mult), "sf")
     g.wait_ge(S.sf, 1)
     g.partition_broadcast(T.selm[:], T.self1[0:1, :], 128).then_inc(S.sm, 1)
     g.wait_ge(S.sm, 1)
-    rb, pb = dst(B)
-    rp, pp = dst(P)
-    g.remote_dma_fused([
-        RemoteDMATransfer(dst_ids=[DstId(rid=rb, pnc=pb)], dma_engine_mask=m_far, remote_sem=S.a_mb,
-                          src=T.selm[:, B:B + 1], dst=T.msgb[:]),
-        RemoteDMATransfer(dst_ids=[DstId(rid=rp, pnc=pp)], dma_engine_mask=m_p, remote_sem=S.a_mp,
-                          src=T.selm[:, P:P + 1], dst=T.msgp[:]),
-    ], local_sem=S.sent)
-    n_sent = [len(eng_far) + len(eng_p)]
-
-    def ship(d, lq, ls, l0, q, s, n, rsem, mask, cnt):
+    for d, msg, rsem, mask in ((B, T.msgb, S.a_mb, m_far), (P, T.msgp, S.a_mp, m_p)):
         rid, pid = dst(d)
-        g.remote_dma(lq[:, l0:l0 + n].bitcast(dt.uint8), q[:, 0:n].bitcast(dt.uint8), rsem, S.sent, pid, rid, mask)
-        g.remote_dma(ls[:, l0:l0 + n], s[:, 0:n], rsem, S.sent, pid, rid, mask)
-        n_sent[0] += 2 * cnt
+        g.remote_dma(msg[:], T.selm[:, d:d + 1], rsem, S.sent, pid, rid, mask)
+    n_sent = [nf + npe]
+
+    def ship(d, lq, ls, l0, q, s, n, rsem):
+        rid, pid = dst(d)
+        g.remote_dma(lq[:, l0:l0 + n].bitcast(dt.uint8), q[:, 0:n].bitcast(dt.uint8), rsem, S.sent, pid, rid, m_far)
+        g.remote_dma(ls[:, l0:l0 + n], s[:, 0:n], rsem, S.sent, pid, rid, m_far)
+        n_sent[0] += 2 * nf
+
+    def ship_bp(lq, ls, q, s, n, from_to):
+        for src, land, codes in ((q, lq, True), (s, ls, False)):
+            tr = []
+            for d, m, (j, l, rs) in zip((B, P), (m_far, m_p), from_to):
+                a, b = src[:, j:j + n], land[:, l:l + n]
+                if codes:
+                    a, b = a.bitcast(dt.uint8), b.bitcast(dt.uint8)
+                rid, pid = dst(d)
+                tr.append(RemoteDMATransfer(dst_ids=[DstId(rid=rid, pnc=pid)], dma_engine_mask=m, remote_sem=rs,
+                                            src=a, dst=b))
+            g.remote_dma_fused(tr, local_sem=S.sent)
+        n_sent[0] += 2 * (nf + npe)
 
     V.wait_ge(S.ld_send, 32)
     for a in range(4):
         vec(V.tensor_scalar(T.off[32 * a:32 * a + 32, :], T.raws[:], 4.0, 0.0, op.mult, op.max), "off")
     V.wait_ge(S.ld_w, 32)
-    vec(V.quantize_mx(T.qe[:], T.se[:], T.wt[:]), "q_e")
-    g.wait_ge(S.q_e, 1)
-    nf, npe = len(eng_far), len(eng_p)
-    ship(A, T.le, T.les, 0, T.qe, T.se, 2 * EX, S.a_e, m_far, nf)
+    vec(V.quantize_mx(T.qw[:], T.sw[:], T.wt[:]), "q_w")
+    g.wait_ge(S.q_w, 1)
+    ship(A, T.le, T.les, E_A, T.qw, T.sw, 2 * EX, S.a_e)
 
+    H = EV // 2
     V.wait_ge(S.bas, 2)
     V.wait_ge(S.sm, 1)
     vec(V.tensor_scalar(T.offo[:], T.base[:], T.selm[:, rank:rank + 1], None, op.add), "offo")
+    vec(V.tensor_scalar(T.sela[:], T.selm[:, A:A + 1], float(SL * (SECOND - A)) / EV, None, op.mult), "sel_a")
     for q in (V, A_):
         q.wait_ge(S.offo, 1)
         q.wait_ge(S.ld_w, 32)
-    H = 2 * EX
     vec(V.tensor_copy(T.ho[:, 0:H], T.wt[:].indirect(T.offo[:, 0:16])), "g_o")
-    vec(A_.activation(T.ho[:, H:2 * H], T.wt[:].indirect(T.offo[:, 16:32]), copy), "g_o")
+    vec(A_.activation(T.ho[:, H:EV], T.wt[:].indirect(T.offo[:, 16:32]), copy), "g_o")
+    V.wait_ge(S.g_o, 2)
+    vec(V.quantize_mx(T.qo[:], T.so[:], T.ho[:]), "q_o")
 
-    def cols(tile, e0, d, ts_v, ts_s, sem):
-        o = T.off[:, 12 * d:12 * d + 12]
-        for t in ts_v:
-            vec(V.tensor_copy(tile[:, e0 + t:e0 + 4 * CAP:4], T.xt[:, t:4 * NX].indirect(o)), sem)
-        for t in ts_s:
-            vec(A_.activation(tile[:, e0 + t:e0 + 4 * CAP:4], T.xt[:, t:4 * NX].indirect(o), copy), sem)
+    def cols(eng, tile, d, k, ts, sem):
+        o = T.off[:, 12 * d:12 * (d + k)]
+        for t in ts:
+            out, win = tile[:, t:k * OV:4], T.xt[:, t:4 * NX].indirect(o)
+            vec(V.tensor_copy(out, win) if eng is V else A_.activation(out, win, copy), sem)
 
     for q in (V, A_):
         q.wait_ge(S.off, 4)
         q.wait_ge(S.ld_x, 16)
-    cols(T.ha, 0, A, (0, 1), (2, 3), "g_a")
+    cols(V, T.ha, A, 1, (0, 1), "g_a")
+    cols(A_, T.ha, A, 1, (2, 3), "g_a")
     V.wait_ge(S.g_a, 4)
     vec(V.quantize_mx(T.qa[:], T.sa[:], T.ha[:]), "q_a")
     g.wait_ge(S.q_a, 1)
-    ship(A, T.lc, T.lcs, L_A, T.qa, T.sa, CAP, S.a_a, m_far, nf)
-
-    cols(T.hp, 4 * EX, P, (0, 1), (2, 3), "g_p")
-    cols(T.hb, 0, B, (0, 1), (2, 3), "g_b")
-    V.wait_ge(S.a_mp, npe)
-    vec(V.tensor_scalar(T.offp[:], T.base[:], T.msgp[:], None, op.add), "offp")
+    ship(A, T.lc, T.lcs, CAP * rank, T.qa, T.sa, CAP, S.a_a)
+    cols(V, T.hbp, bp, 2, (0, 1), "g_bp")
+    cols(A_, T.hbp, bp, 2, (2, 3), "g_bp")
+    V.wait_ge(S.g_bp, 4)
+    vec(V.quantize_mx(T.qbp[:], T.sbp[:], T.hbp[:]), "q_bp")
+    g.wait_ge(S.q_bp, 1)
+    ship_bp(T.lc, T.lcs, T.qbp, T.sbp, CAP, ((jb, CAP * rank, S.a_b), (jp, CAP * rank, S.a_p)))
+    cols(A_, T.hx, rank, 1, (0, 1), "g_x")
     V.wait_ge(S.a_mb, nf)
     vec(V.tensor_scalar(T.offb[:], T.base[:], T.msgb[:], None, op.add), "offb")
-    V.wait_ge(S.offp, 1)
-    A_.wait_ge(S.offp, 1)
-    vec(V.tensor_copy(T.hp[:, 0:H], T.wt[:].indirect(T.offp[:, 0:16])), "g_p")
-    vec(A_.activation(T.hp[:, H:2 * H], T.wt[:].indirect(T.offp[:, 16:32]), copy), "g_p")
+    V.wait_ge(S.a_mp, npe)
+    vec(V.tensor_scalar(T.offp[:], T.base[:], T.msgp[:], None, op.add), "offp")
     A_.wait_ge(S.offb, 1)
-    vec(A_.activation(T.hb[:, 4 * CAP:4 * RUN], T.wt[:].indirect(T.offb[:]), copy), "g_b")
-    V.wait_ge(S.g_p, 6)
-    vec(V.quantize_mx(T.qp[:], T.sp[:], T.hp[:]), "q_p")
-    g.wait_ge(S.q_p, 1)
-    ship(P, T.lc, T.lcs, L_EP, T.qp, T.sp, RUN, S.a_p, m_p, npe)
-    V.wait_ge(S.g_b, 5)
-    vec(V.quantize_mx(T.qb[:], T.sb[:], T.hb[:]), "q_b")
-    g.wait_ge(S.q_b, 1)
-    ship(B, T.lc, T.lcs, L_B, T.qb, T.sb, RUN, S.a_b, m_far, nf)
-    cols(T.hx, 0, rank, (0, 1), (2, 3), "g_x")
-    V.wait_ge(S.g_o, 2)
-    vec(V.quantize_mx(T.qo[:], T.so[:], T.ho[:]), "q_o")
+    vec(A_.activation(T.he[:, 0:EV], T.wt[:].indirect(T.offb[:]), copy), "g_e")
+    V.wait_ge(S.offp, 1)
+    vec(V.tensor_copy(T.he[:, EV:2 * EV], T.wt[:].indirect(T.offp[:])), "g_e")
+    V.wait_ge(S.g_e, 2)
+    vec(V.quantize_mx(T.qe[:], T.se[:], T.he[:]), "q_e")
+    g.wait_ge(S.q_e, 1)
+    ship_bp(T.le, T.les, T.qe, T.se, EX, ((0, E_B, S.a_eb), (EX, E_P, S.a_ep)))
+    cols(A_, T.hx, rank, 1, (2,), "g_x")
+    cols(V, T.hx, rank, 1, (3,), "g_x")
     V.wait_ge(S.g_x, 4)
-    vec(V.quantize_mx(T.lc[:, L_O:L_O + CAP], T.lcs[:, L_O:L_O + CAP], T.hx[:]), "q_x")
+    vec(V.quantize_mx(T.lc[:, CAP * rank:CAP * rank + CAP], T.lcs[:, CAP * rank:CAP * rank + CAP], T.hx[:]), "q_x")
 
-    pos = {P: 0, rank: 1, A: 2, B: 3}
-    blk = {rank: BL_O, A: BL_A, P: BL_P, B: BL_B}
     V.wait_ge(S.ld_pl, 64)
-    vec(V.tensor_scalar(T.sela[:], T.selm[:, A:A + 1], float(SL) / (4 * EX), None, op.mult), "sel_a")
-    vec(V.tensor_scalar(T.tm[:, 0:32], T.rawp[:], float(CAP * pos[0] + SL * blk[0]), None, op.add), "tmd")
-    for k in range(1, 4):
-        vec(V.tensor_scalar(T.tm[:, 32 * k:32 * k + 32], T.rawp[:], float(CAP * k),
-                            float(CAP * (pos[k] - pos[k - 1] - 1)), op.is_ge, op.mult), "tmd")
-        vec(V.tensor_scalar(T.tm[:, 96 + 32 * k:128 + 32 * k], T.rawo[:], float(k),
-                            float(SL * (blk[k] - blk[k - 1])), op.is_ge, op.mult), "tmd")
+    vec(V.tensor_scalar(T.t1[:], T.rawo[:], float(SL), None, op.mult), "t1d")
     V.wait_ge(S.sel_a, 1)
-    vec(V.tensor_scalar(T.tm[:, 224:256], T.rawo[:], float(A), T.sela[0:32, :], op.is_equal, op.mult), "tmd")
-    V.wait_ge(S.tmd, 8)
-    vec(V.tensor_tensor(T.tn[:], T.tm[:, 0:128], T.tm[:, 128:256], op.add), "tnd")
-    V.wait_ge(S.tnd, 1)
-    vec(V.tensor_tensor(T.to[:], T.tn[:, 0:64], T.tn[:, 64:128], op.add), "tod")
-    V.wait_ge(S.tod, 1)
-    vec(V.tensor_tensor(T.tp[:], T.to[:, 0:32], T.to[:, 32:64], op.add), "tpd")
-    V.wait_ge(S.tpd, 1)
+    vec(V.tensor_scalar(T.t2[:], T.rawo[:], float(A), T.sela[0:32, :], op.is_equal, op.mult), "t2d")
+    V.wait_ge(S.t1d, 1)
+    vec(V.tensor_tensor(T.t3[:], T.t1[:], T.rawp[:], op.add), "t3d")
+    V.wait_ge(S.t2d, 1)
+    V.wait_ge(S.t3d, 1)
+    vec(V.tensor_tensor(T.t4[:], T.t3[:], T.t2[:], op.add), "t4d")
+    V.wait_ge(S.t4d, 1)
     for a in range(4):
-        vec(V.tensor_copy(T.offy[32 * a:32 * a + 32, :], T.tp[:]), "offy")
+        vec(V.tensor_copy(T.offy[32 * a:32 * a + 32, :], T.t4[:]), "offy")
 
-    own = (T.qo, T.so, 0, BL_O)
-    a0 = (T.le, T.les, 0, BL_A)
-    a1 = (T.le, T.les, EX, BL_A + 1)
-    ep = (T.lc, T.lcs, L_EP, BL_P)
-    eb = (T.lc, T.lcs, L_EB, BL_B)
+    own = (T.qo, T.so, 0, rank)
+    a0 = (T.le, T.les, E_A, A)
+    a1 = (T.le, T.les, E_A + EX, SECOND)
+    eb = (T.le, T.les, E_B, B)
+    ep = (T.le, T.les, E_P, P)
     nmm = [0]
 
-    def prod(e, c0, c1, bank, eng, ev):
+    def prod(e, d, bank, eng, ev):
         q, s, j, b = e
-        k = nmm[0]
+        sem = S["mm%d" % nmm[0]]
         nmm[0] += 1
+        c0, n = CAP * d, 2 * CAP
         ps = T["ps%d" % bank]
-        sem = S["mm%d" % k]
-        TE.matmul_mx(ps[:, 0:c1 - c0], q[:, j:j + EX], s[:, j:j + EX], T.lc[:, c0:c1], T.lcs[:, c0:c1],
+        TE.matmul_mx(ps[:, 0:n], q[:, j:j + EX], s[:, j:j + EX], T.lc[:, c0:c0 + n], T.lcs[:, c0:c0 + n],
                      True, True).then_inc(sem, 1)
-        w0 = SL * b + c0 - L_P
+        w0 = SL * b + c0
         eng.wait_ge(sem, 1)
         if eng is V:
-            V.tensor_copy(T.win[:, w0:w0 + c1 - c0], ps[:, 0:c1 - c0]).then_inc(S[ev], 1)
+            V.tensor_copy(T.win[:, w0:w0 + n], ps[:, 0:n]).then_inc(S[ev], 1)
         else:
-            A_.activation(T.win[:, w0:w0 + c1 - c0], ps[:, 0:c1 - c0], copy).then_inc(S[ev], 1)
+            A_.activation(T.win[:, w0:w0 + n], ps[:, 0:n], copy).then_inc(S[ev], 1)
 
     TE.wait_ge(S.q_o, 1)
     TE.wait_ge(S.q_x, 1)
     TE.wait_ge(S.a_e, 2 * nf)
     TE.wait_ge(S.a_a, 2 * nf)
-    prod(own, L_O, L_B, 0, A_, "ev1")
-    prod(a0, L_O, L_B, 1, V, "ev1")
-    prod(a1, L_O, L_B, 2, A_, "ev1")
-    TE.wait_ge(S.a_p, 2 * npe)
-    mid = L_P + 3 * CAP // 2
-    prod(ep, L_P, mid, 6, V, "ev2")
-    prod(ep, mid, L_B, 7, A_, "ev2")
-    prod(own, L_P, L_O, 3, V, "ev2")
-    prod(a0, L_P, L_O, 4, A_, "ev2")
-    prod(a1, L_P, L_O, 5, V, "ev2")
+    prod(own, oa, 0, A_, "ev1")
+    prod(a0, oa, 1, V, "ev1")
+    prod(a1, oa, 2, A_, "ev1")
     TE.wait_ge(S.a_b, 2 * nf)
+    TE.wait_ge(S.a_p, 2 * npe)
+    prod(own, bp, 3, V, "ev2")
+    prod(a0, bp, 4, A_, "ev2")
+    prod(a1, bp, 5, V, "ev2")
+    TE.wait_ge(S.a_ep, 2 * npe)
+    prod(ep, oa, 6, A_, "ev3")
+    prod(ep, bp, 7, V, "ev3")
     TE.wait_ge(S.ev1, 3)
-    prod(eb, L_P, L_A, 0, V, "ev3")
-    prod(eb, L_A, L_EB, 1, A_, "ev3")
-    prod(own, L_B, L_EB, 2, V, "ev3")
-    TE.wait_ge(S.ev2, 5)
-    prod(a0, L_B, L_EB, 3, A_, "ev3")
-    prod(a1, L_B, L_EB, 4, V, "ev3")
-    prod(ep, L_B, L_EB, 5, A_, "ev3")
+    TE.wait_ge(S.a_eb, 2 * nf)
+    prod(eb, oa, 0, A_, "ev4")
+    prod(eb, bp, 1, V, "ev4")
 
     for q in (V, A_):
         q.wait_ge(S.offy, 4)
         q.wait_ge(S.ev1, 3)
-        q.wait_ge(S.ev2, 5)
-        q.wait_ge(S.ev3, 6)
+        q.wait_ge(S.ev2, 3)
+        q.wait_ge(S.ev3, 2)
+        q.wait_ge(S.ev4, 2)
     h = NX // 2
     V.tensor_copy(T.yt[:, 0:h], T.win[:].indirect(T.offy[:, 0:16])).then_inc(S.g_y1, 1)
     A_.activation(T.yt[:, h:NX], T.win[:].indirect(T.offy[:, 16:32]), copy).then_inc(S.g_y2, 1)

from concourse.bass import DstId, RemoteDMATransfer
from concourse.mybir import dt, AluOpType, ActivationFunctionType

CAP = 192
NX = 512
EX = 128
SL = 4 * CAP
EV, OV = 4 * EX, 4 * CAP

E_A, E_B, E_P = 0, 2 * EX, 3 * EX
SECOND = 4

CODE = "float8_e4m3fn_x4"
SCRATCH = {
    "raws": ("sbuf", [32, 48], "int32"),
    "rawp": ("sbuf", [32, 32], "int32"),
    "rawo": ("sbuf", [32, 32], "int32"),
    "selr": ("sbuf", [128, 16], "int32"),
    "self1": ("sbuf", [128, 16], "float32"),
    "selm": ("sbuf", [128, 16], "float32"),
    "sela": ("sbuf", [128, 1], "float32"),
    "ia": ("sbuf", [128, 32], "int32"),
    "ib": ("sbuf", [128, 32], "int32"),
    "ic": ("sbuf", [128, 32], "int32"),
    "base": ("sbuf", [128, 32], "float32"),
    "off": ("sbuf", [128, 48], "uint16"),
    "offo": ("sbuf", [128, 32], "uint16"),
    "offp": ("sbuf", [128, 32], "uint16"),
    "offb": ("sbuf", [128, 32], "uint16"),
    "offy": ("sbuf", [128, 32], "uint16"),
    "t1": ("sbuf", [32, 32], "float32"),
    "t2": ("sbuf", [32, 32], "float32"),
    "t3": ("sbuf", [32, 32], "float32"),
    "t4": ("sbuf", [32, 32], "float32"),
    "msgp": ("sbuf", [128, 1], "float32"),
    "msgb": ("sbuf", [128, 1], "float32"),
    "xt": ("sbuf", [128, 4 * NX], "bfloat16"),
    "wt": ("sbuf", [128, 2 * EV], "bfloat16"),
    "ho": ("sbuf", [128, EV], "bfloat16"),
    "he": ("sbuf", [128, 2 * EV], "bfloat16"),
    "ha": ("sbuf", [128, OV], "bfloat16"),
    "hbp": ("sbuf", [128, 2 * OV], "bfloat16"),
    "hx": ("sbuf", [128, OV], "bfloat16"),
    "qw": ("sbuf", [128, 2 * EX], CODE), "sw": ("sbuf", [128, 2 * EX], "uint8"),
    "qe": ("sbuf", [128, 2 * EX], CODE), "se": ("sbuf", [128, 2 * EX], "uint8"),
    "qo": ("sbuf", [128, EX], CODE), "so": ("sbuf", [128, EX], "uint8"),
    "qa": ("sbuf", [128, CAP], CODE), "sa": ("sbuf", [128, CAP], "uint8"),
    "qbp": ("sbuf", [128, 2 * CAP], CODE), "sbp": ("sbuf", [128, 2 * CAP], "uint8"),
    "le": ("sbuf", [128, 4 * EX], CODE), "les": ("sbuf", [128, 4 * EX], "uint8"),
    "lc": ("sbuf", [128, SL], CODE), "lcs": ("sbuf", [128, SL], "uint8"),
    "win": ("sbuf", [128, 5 * SL], "float32"),
    "yt": ("sbuf", [128, NX], "float32"),
}
for _k in range(8):
    SCRATCH["ps%d" % _k] = ("psum", [128, 512], "float32")

SEMAPHORES = ["ld_sel", "ld_send", "ld_w", "ld_x", "ld_pl", "st_a", "st_b",
              "io", "io2", "bas", "sf", "sm", "off", "offo", "offp", "offb", "offy", "sel_a",
              "t1d", "t2d", "t3d", "t4d",
              "q_w", "q_e", "q_o", "q_a", "q_bp", "q_x",
              "g_o", "g_a", "g_bp", "g_e", "g_x", "g_y1", "g_y2",
              "sent", "a_mp", "a_mb", "a_e", "a_a", "a_p", "a_b", "a_eb", "a_ep",
              "ev1", "ev2", "ev3", "ev4"] + ["mm%d" % k for k in range(10)]


def rank_program(g, core, T, topo):
    rank = T.rank_of(core)
    if rank is None:
        return
    S = T.sem
    V, A_, TE, SY = g.vector, g.scalar, g.tensor, g.sync
    op = AluOpType
    copy = ActivationFunctionType.Copy

    others = [d for d in range(len(T.cores)) if d != rank]
    P = [d for d in others if topo.chip(T.cores[d]) == topo.chip(core)][0]
    far = [d for d in others if d != P]
    A = [d for d in far if topo.die(T.cores[d]) == topo.die(core)][0]
    B = [d for d in far if d != A][0]
    assert abs(rank - A) == 1 and abs(B - P) == 1
    oa, bp = min(rank, A), min(B, P)
    jb, jp = CAP * (B - bp), CAP * (P - bp)
    eng_far = topo.engines(core, T.cores[B])
    eng_p = [e for e in topo.engines(core, T.cores[P]) if e not in eng_far]
    m_far = sum(1 << e for e in eng_far)
    m_p = sum(1 << e for e in eng_p)
    nf, npe = len(eng_far), len(eng_p)

    def dst(d):
        rid, pid, _ = topo.addr(T.cores[d])
        return rid, pid

    def vec(inst, sem, n=1):
        inst.then_inc(S[sem], n)

    SY.dma_start(T.selr[0:1, 0:16], T.sel[:]).then_inc(S.ld_sel, 16)
    A_.dma_start(T.raws[16:32, :], T.send[:]).then_inc(S.ld_send, 16)
    SY.dma_start(T.raws[0:16, :], T.send[:]).then_inc(S.ld_send, 16)
    A_.dma_start(T.rawp[0:16, :], T.place[:]).then_inc(S.ld_pl, 16)
    SY.dma_start(T.rawp[16:32, :], T.place[:]).then_inc(S.ld_pl, 16)
    A_.dma_start(T.rawo[0:16, :], T.of[:]).then_inc(S.ld_pl, 16)
    for k in range(2):
        SY.dma_start(T.wt[:, EV * k:EV * k + EV], T.w[128 * k:128 * k + 128, :]).then_inc(S.ld_w, 16)
    A_.dma_start(T.rawo[16:32, :], T.of[:]).then_inc(S.ld_pl, 16)
    SY.dma_start(T.xt[:], T.x[:]).then_inc(S.ld_x, 16)

    g.iota(T.ia[:], [[16, 32]], 0, 1).then_inc(S["io"], 1)
    g.iota(T.ic[:], [[16, 32]], 0, 0).then_inc(S.io2, 1)
    V.wait_ge(S["io"], 1)
    vec(V.tensor_scalar(T.ib[:], T.ia[:], 15, None, op.bitwise_and), "bas")
    V.wait_ge(S["bas"], 1)
    V.wait_ge(S.io2, 1)
    vec(V.tensor_tensor(T.base[:], T.ib[:], T.ic[:], op.add), "bas")

    V.wait_ge(S.ld_sel, 16)
    vec(V.tensor_scalar(T.self1[0:1, :], T.selr[0:1, :], 0.0, float(EV), op.max, op.mult), "sf")
    g.wait_ge(S.sf, 1)
    g.partition_broadcast(T.selm[:], T.self1[0:1, :], 128).then_inc(S.sm, 1)
    g.wait_ge(S.sm, 1)
    for d, msg, rsem, mask in ((B, T.msgb, S.a_mb, m_far), (P, T.msgp, S.a_mp, m_p)):
        rid, pid = dst(d)
        g.remote_dma(msg[:], T.selm[:, d:d + 1], rsem, S.sent, pid, rid, mask)
    n_sent = [nf + npe]

    def ship(d, lq, ls, l0, q, s, n, rsem):
        rid, pid = dst(d)
        g.remote_dma(lq[:, l0:l0 + n].bitcast(dt.uint8), q[:, 0:n].bitcast(dt.uint8), rsem, S.sent, pid, rid, m_far)
        g.remote_dma(ls[:, l0:l0 + n], s[:, 0:n], rsem, S.sent, pid, rid, m_far)
        n_sent[0] += 2 * nf

    def ship_bp(lq, ls, q, s, n, from_to):
        for src, land, codes in ((q, lq, True), (s, ls, False)):
            tr = []
            for d, m, (j, l, rs) in zip((B, P), (m_far, m_p), from_to):
                a, b = src[:, j:j + n], land[:, l:l + n]
                if codes:
                    a, b = a.bitcast(dt.uint8), b.bitcast(dt.uint8)
                rid, pid = dst(d)
                tr.append(RemoteDMATransfer(dst_ids=[DstId(rid=rid, pnc=pid)], dma_engine_mask=m, remote_sem=rs,
                                            src=a, dst=b))
            g.remote_dma_fused(tr, local_sem=S.sent)
        n_sent[0] += 2 * (nf + npe)

    V.wait_ge(S.ld_send, 32)
    for a in range(4):
        vec(V.tensor_scalar(T.off[32 * a:32 * a + 32, :], T.raws[:], 4.0, 0.0, op.mult, op.max), "off")
    V.wait_ge(S.ld_w, 32)
    vec(V.quantize_mx(T.qw[:], T.sw[:], T.wt[:]), "q_w")
    g.wait_ge(S.q_w, 1)
    ship(A, T.le, T.les, E_A, T.qw, T.sw, 2 * EX, S.a_e)

    H = EV // 2
    V.wait_ge(S.bas, 2)
    V.wait_ge(S.sm, 1)
    vec(V.tensor_scalar(T.offo[:], T.base[:], T.selm[:, rank:rank + 1], None, op.add), "offo")
    vec(V.tensor_scalar(T.sela[:], T.selm[:, A:A + 1], float(SL * (SECOND - A)) / EV, None, op.mult), "sel_a")
    for q in (V, A_):
        q.wait_ge(S.offo, 1)
        q.wait_ge(S.ld_w, 32)
    vec(V.tensor_copy(T.ho[:, 0:H], T.wt[:].indirect(T.offo[:, 0:16])), "g_o")
    vec(A_.activation(T.ho[:, H:EV], T.wt[:].indirect(T.offo[:, 16:32]), copy), "g_o")
    V.wait_ge(S.g_o, 2)
    vec(V.quantize_mx(T.qo[:], T.so[:], T.ho[:]), "q_o")

    def cols(eng, tile, d, k, ts, sem):
        o = T.off[:, 12 * d:12 * (d + k)]
        for t in ts:
            out, win = tile[:, t:k * OV:4], T.xt[:, t:4 * NX].indirect(o)
            vec(V.tensor_copy(out, win) if eng is V else A_.activation(out, win, copy), sem)

    for q in (V, A_):
        q.wait_ge(S.off, 4)
        q.wait_ge(S.ld_x, 16)
    cols(V, T.ha, A, 1, (0, 1), "g_a")
    cols(A_, T.ha, A, 1, (2, 3), "g_a")
    V.wait_ge(S.g_a, 4)
    vec(V.quantize_mx(T.qa[:], T.sa[:], T.ha[:]), "q_a")
    g.wait_ge(S.q_a, 1)
    ship(A, T.lc, T.lcs, CAP * rank, T.qa, T.sa, CAP, S.a_a)
    cols(V, T.hbp, bp, 2, (0, 1), "g_bp")
    cols(A_, T.hbp, bp, 2, (2, 3), "g_bp")
    V.wait_ge(S.g_bp, 4)
    vec(V.quantize_mx(T.qbp[:], T.sbp[:], T.hbp[:]), "q_bp")
    g.wait_ge(S.q_bp, 1)
    ship_bp(T.lc, T.lcs, T.qbp, T.sbp, CAP, ((jb, CAP * rank, S.a_b), (jp, CAP * rank, S.a_p)))
    cols(A_, T.hx, rank, 1, (0, 1), "g_x")
    V.wait_ge(S.a_mb, nf)
    vec(V.tensor_scalar(T.offb[:], T.base[:], T.msgb[:], None, op.add), "offb")
    V.wait_ge(S.a_mp, npe)
    vec(V.tensor_scalar(T.offp[:], T.base[:], T.msgp[:], None, op.add), "offp")
    A_.wait_ge(S.offb, 1)
    vec(A_.activation(T.he[:, 0:EV], T.wt[:].indirect(T.offb[:]), copy), "g_e")
    V.wait_ge(S.offp, 1)
    vec(V.tensor_copy(T.he[:, EV:2 * EV], T.wt[:].indirect(T.offp[:])), "g_e")
    V.wait_ge(S.g_e, 2)
    vec(V.quantize_mx(T.qe[:], T.se[:], T.he[:]), "q_e")
    g.wait_ge(S.q_e, 1)
    ship_bp(T.le, T.les, T.qe, T.se, EX, ((0, E_B, S.a_eb), (EX, E_P, S.a_ep)))
    cols(A_, T.hx, rank, 1, (2,), "g_x")
    cols(V, T.hx, rank, 1, (3,), "g_x")
    V.wait_ge(S.g_x, 4)
    vec(V.quantize_mx(T.lc[:, CAP * rank:CAP * rank + CAP], T.lcs[:, CAP * rank:CAP * rank + CAP], T.hx[:]), "q_x")

    V.wait_ge(S.ld_pl, 64)
    vec(V.tensor_scalar(T.t1[:], T.rawo[:], float(SL), None, op.mult), "t1d")
    V.wait_ge(S.sel_a, 1)
    vec(V.tensor_scalar(T.t2[:], T.rawo[:], float(A), T.sela[0:32, :], op.is_equal, op.mult), "t2d")
    V.wait_ge(S.t1d, 1)
    vec(V.tensor_tensor(T.t3[:], T.t1[:], T.rawp[:], op.add), "t3d")
    V.wait_ge(S.t2d, 1)
    V.wait_ge(S.t3d, 1)
    vec(V.tensor_tensor(T.t4[:], T.t3[:], T.t2[:], op.add), "t4d")
    V.wait_ge(S.t4d, 1)
    for a in range(4):
        vec(V.tensor_copy(T.offy[32 * a:32 * a + 32, :], T.t4[:]), "offy")

    own = (T.qo, T.so, 0, rank)
    a0 = (T.le, T.les, E_A, A)
    a1 = (T.le, T.les, E_A + EX, SECOND)
    eb = (T.le, T.les, E_B, B)
    ep = (T.le, T.les, E_P, P)
    nmm = [0]

    def prod(e, d, bank, eng, ev):
        q, s, j, b = e
        sem = S["mm%d" % nmm[0]]
        nmm[0] += 1
        c0, n = CAP * d, 2 * CAP
        ps = T["ps%d" % bank]
        TE.matmul_mx(ps[:, 0:n], q[:, j:j + EX], s[:, j:j + EX], T.lc[:, c0:c0 + n], T.lcs[:, c0:c0 + n],
                     True, True).then_inc(sem, 1)
        w0 = SL * b + c0
        eng.wait_ge(sem, 1)
        if eng is V:
            V.tensor_copy(T.win[:, w0:w0 + n], ps[:, 0:n]).then_inc(S[ev], 1)
        else:
            A_.activation(T.win[:, w0:w0 + n], ps[:, 0:n], copy).then_inc(S[ev], 1)

    TE.wait_ge(S.q_o, 1)
    TE.wait_ge(S.q_x, 1)
    TE.wait_ge(S.a_e, 2 * nf)
    TE.wait_ge(S.a_a, 2 * nf)
    prod(own, oa, 0, A_, "ev1")
    prod(a0, oa, 1, V, "ev1")
    prod(a1, oa, 2, A_, "ev1")
    TE.wait_ge(S.a_b, 2 * nf)
    TE.wait_ge(S.a_p, 2 * npe)
    prod(own, bp, 3, V, "ev2")
    prod(a0, bp, 4, A_, "ev2")
    prod(a1, bp, 5, V, "ev2")
    TE.wait_ge(S.a_ep, 2 * npe)
    prod(ep, oa, 6, A_, "ev3")
    prod(ep, bp, 7, V, "ev3")
    TE.wait_ge(S.ev1, 3)
    TE.wait_ge(S.a_eb, 2 * nf)
    prod(eb, oa, 0, A_, "ev4")
    prod(eb, bp, 1, V, "ev4")

    for q in (V, A_):
        q.wait_ge(S.offy, 4)
        q.wait_ge(S.ev1, 3)
        q.wait_ge(S.ev2, 3)
        q.wait_ge(S.ev3, 2)
        q.wait_ge(S.ev4, 2)
    h = NX // 2
    V.tensor_copy(T.yt[:, 0:h], T.win[:].indirect(T.offy[:, 0:16])).then_inc(S.g_y1, 1)
    A_.activation(T.yt[:, h:NX], T.win[:].indirect(T.offy[:, 16:32]), copy).then_inc(S.g_y2, 1)
    SY.wait_ge(S.g_y1, 1)
    SY.dma_start(T.y[:, 0:h], T.yt[:, 0:h]).then_inc(S.st_a, 16)
    A_.wait_ge(S.g_y2, 1)
    A_.dma_start(T.y[:, h:NX], T.yt[:, h:NX]).then_inc(S.st_b, 16)
    SY.wait_ge(S.st_a, 16)
    A_.wait_ge(S.st_b, 16)
    g.wait_ge(S.sent, n_sent[0])
